import numpy as np
import ml_dtypes


def mxq(x, axis, fmt="e4m3"):
    dtype, down = {"e4m3": (ml_dtypes.float8_e4m3fn, 7), "e5m2": (ml_dtypes.float8_e5m2, 14)}[fmt]
    v = np.moveaxis(np.asarray(x, np.float32).astype(ml_dtypes.bfloat16).astype(np.float64), axis, -1)
    blocks = v.reshape(v.shape[:-1] + (-1, 32))
    amax = np.abs(blocks).max(-1, keepdims=True)
    byte = np.maximum(np.where(amax > 0, np.frexp(amax)[1] - 1 + 127, 0) - down, 1)
    scale = np.exp2(byte - 127.0)
    codes = (blocks / scale).astype(np.float32).astype(dtype).astype(np.float64)
    return np.moveaxis((codes * scale).reshape(v.shape), -1, axis)


WIDE = False


def mx_kscale(k):
    if not WIDE:
        return np.ones(k)
    levels = np.array([24, -24, 12, -12, 0])
    if k % 512:
        return np.exp2(np.random.permutation(np.resize(levels, k // 32))).repeat(32)
    a = np.empty((k // 512, 16))
    for p in range(k // 512):
        a[p, :8] = np.random.permutation(np.resize(levels, 8))
        for g in range(8):
            far = levels[np.abs(levels - a[p, g]) >= 10]
            a[p, g + 8] = far[np.random.randint(len(far))]
    return np.exp2(a.ravel()).repeat(32)


def f64(x):
    return np.asarray(x).astype(np.float64)


E2M1 = np.array([0.0, 0.5, 1.0, 1.5, 2.0, 3.0, 4.0, 6.0, -0.0, -0.5, -1.0, -1.5, -2.0, -3.0, -4.0, -6.0])


def pack_weight(w, fmt):
    k, n = w.shape
    w = f64(np.asarray(w, np.float32).astype(ml_dtypes.bfloat16)).reshape(k // 32, 32, n)
    amax = np.abs(w).max(1)
    if fmt == "e4m3":
        byte = np.frexp(amax)[1] - 1 + 127 - 7
    else:
        mant, ex = np.frexp(amax / 6.0)
        byte = np.where(mant > 0.5, ex, ex - 1) + 127
    byte = np.clip(np.where(amax > 0, byte, 1), 1, 254)
    scaled = (w * np.exp2(127.0 - byte)[:, None, :]).reshape(k, n).astype(np.float32)
    by_word = np.ascontiguousarray(scaled.reshape(k // 512, 128, 4, n).transpose(0, 1, 3, 2))
    if fmt == "e4m3":
        words = by_word.astype(ml_dtypes.float8_e4m3fn).view(np.uint8)
    else:
        c = by_word.astype(ml_dtypes.float4_e2m1fn).view(np.uint8) & 0xF
        words = (c[..., 0::2] | (c[..., 1::2] << 4)).reshape(k // 512, 128, 2 * n)
    return np.ascontiguousarray(words), np.ascontiguousarray(byte.astype(np.uint8).reshape(k // 512, 16, n))


def unpack_weight(words, scales, fmt):
    g, _, n = scales.shape
    words = np.ascontiguousarray(words).reshape(g, 128, n, -1)
    if fmt == "e4m3":
        vals = words.view(ml_dtypes.float8_e4m3fn).astype(np.float64)
    else:
        nib = np.empty((g, 128, n, 4), np.uint8)
        nib[..., 0::2] = words & 0xF
        nib[..., 1::2] = words >> 4
        vals = E2M1[nib]
    vals = vals * np.repeat(np.exp2(scales.astype(np.float64) - 127.0), 8, axis=1)[..., None]
    return vals.transpose(0, 1, 3, 2).reshape(g * 512, n)


K, J, N, T = 1024, 1024, 256, 1024


def setup_inputs():
    n = np.random.standard_normal
    u = mx_kscale(J)[:, None]
    s = mx_kscale(K)[:, None]
    x = n((K, T)); x[:512] *= 6.0
    w = n((K, J)) / np.sqrt(K) / s * 0.4; w[:512] /= 2.0
    v = n((J, N)) / np.sqrt(J) / u
    p_w8 = pack_weight(w[:512], "e4m3")
    p_w4 = pack_weight(w[512:], "e2m1")
    p_v8 = pack_weight(v[:512], "e4m3")
    p_v4 = pack_weight(v[512:], "e2m1")
    return {
        "x": (x * s).astype(np.float32),
        "w8_words": p_w8[0],
        "w8_scales": p_w8[1],
        "w4_words": p_w4[0],
        "w4_scales": p_w4[1],
        "cw": (np.random.uniform(0.5, 2.0, J) * u[:, 0]).astype(np.float32),
        "cb": (0.3 * n(J)).astype(np.float32),
        "v8_words": p_v8[0],
        "v8_scales": p_v8[1],
        "v4_words": p_v4[0],
        "v4_scales": p_v4[1],
        "res": (n((N, T))).astype(np.float32),
    }


def reference(x, w8_words, w8_scales, w4_words, w4_scales, cw, cb, v8_words, v8_scales, v4_words, v4_scales, res):
    x_ = mxq(f64(x), 0, "e4m3")
    w8_ = unpack_weight(w8_words, w8_scales, "e4m3")
    w4_ = unpack_weight(w4_words, w4_scales, "e2m1")
    d = w8_.T @ x_[:512] + w4_.T @ x_[512:]
    h = f64(cw)[:, None] * np.tanh(d + f64(cb)[:, None])
    h_ = mxq(h, 0, "e4m3")
    v8_ = unpack_weight(v8_words, v8_scales, "e4m3")
    v4_ = unpack_weight(v4_words, v4_scales, "e2m1")
    y = v8_.T @ h_[:512] + v4_.T @ h_[512:]
    return f64(res) + y

@@ -1,0 +1,344 @@
+from contextlib import ExitStack
+
+import concourse.mybir as mybir
+
+K, J, N, T = 1024, 1024, 256, 1024
+FLOPS = 2 * K * J * T + 2 * J * N * T
+
+F32 = mybir.dt.float32
+BF16 = mybir.dt.bfloat16
+I32 = mybir.dt.int32
+U32 = mybir.dt.uint32
+U8 = mybir.dt.uint8
+FP8X4 = mybir.dt.float8_e4m3fn_x4
+FP4X4 = mybir.dt.float4_e2m1fn_x4
+ACT = mybir.ActivationFunctionType
+ALU = mybir.AluOpType
+
+P = 128
+PACK = 4
+PASS = P * PACK
+FP8_ROW = 4
+WIDTHS = [256,256,256,128,128]
+RES_SPLIT = 1
+XV = 4
+SPLIT = 4
+WB = 99
+WBONLY = 1
+ORDER = 1
+GS = 0
+RESAT = 9
+EARLY = 1
+N0 = 4
+N1 = 0
+PRE = 3
+SHARE = [4, 8, 16, 16, 4, 4, 0]
+S3 = 6
+WARM0 = 6
+WARM1 = 4
+XV0 = 2
+XS = 8
+OL = 1
+ADD0 = 4
+
+
+def tile_mix_kern_outl_tanh_mix_res_kernel(
+    tc, x, w8_words, w8_scales, w4_words, w4_scales, cw, cb, v8_words, v8_scales, v4_words, v4_scales, res, out
+):
+    nc = tc.nc
+    chunks = len(WIDTHS)
+    starts = [sum(WIDTHS[:c]) for c in range(chunks + 1)]
+
+    with ExitStack() as ctx:
+        sb = ctx.enter_context(tc.tile_pool(name="sb", bufs=1))
+        d_psum = ctx.enter_context(tc.psum_pool(name="d_psum", bufs=6))
+        y_psum = ctx.enter_context(tc.psum_pool(name="y_psum", bufs=2))
+        ctx.enter_context(tc.manual_schedule())
+
+        def keep(name, shape, dtype):
+            return sb.tile(shape, dtype, name=name, align_bytes=64)
+
+        w8_raw = [keep("w8_raw%d" % b, [P, PASS], U32) for b in range(2)]
+        w8 = [keep("w8_%d" % b, [P, PASS], U32) for b in range(2)]
+        w4_raw = [keep("w4_raw%d" % b, [P, 2 * PASS], U8) for b in range(2)]
+        w4 = [keep("w4_%d" % b, [P, 2 * PASS], U8) for b in range(2)]
+        w_sc_raw = keep("w_sc_raw", [P, J], U8)
+        w_sc = keep("w_sc", [P, J], U8)
+        v8 = keep("v8", [P, N], U32)
+        v4 = keep("v4", [P, 2 * N], U8)
+        v_sc = keep("v_sc", [P, N], U8)
+        cb_sb = keep("cb_sb", [P, 2, PACK], F32)
+        cw_sb = keep("cw_sb", [P, 2, PACK], F32)
+        warm_in = keep("warm_in", [P, 1], F32)
+        warm_out = keep("warm_out", [P, 1], F32)
+
+        def per_half(name, cols, dtype):
+            return [[keep("%s%d_%d" % (name, c, a), [P, cols * WIDTHS[c]], dtype) for a in range(2)] for c in range(chunks)]
+
+        x_raw = per_half("x_raw", PACK, F32)
+        x_bf = per_half("x_bf", PACK, BF16)
+        x_q = per_half("x_q", 1, U32)
+        x_sc = per_half("x_sc", 1, U8)
+        th = per_half("th", PACK, F32)
+        h_bf = per_half("h_bf", PACK, BF16)
+        h_rows = per_half("h_rows", PACK, BF16)
+        h_q = per_half("h_q", 1, U32)
+        h_sc = per_half("h_sc", 1, U8)
+        res_edges = [0, starts[RES_SPLIT], T]
+        res_sb = [keep("res%d" % r, [P, 2, res_edges[r + 1] - res_edges[r]], F32) for r in range(2)]
+        out_sb = [keep("out%d" % c, [P, 2, WIDTHS[c]], F32) for c in range(chunks)]
+
+        def load_scales(plane, row, scales, q, queue):
+            if True:
+                queue.dma_start(
+                    out=plane[32 * q + row : 32 * q + row + 4, :].bitcast(I32),
+                    in_=scales[0, 4 * q : 4 * q + 4, :].bitcast(I32),
+                )
+
+        def load_x(c, a):
+            rows = x[a * PASS : (a + 1) * PASS, starts[c] : starts[c + 1]]
+            nc.sync.dma_start(
+                out=x_raw[c][a][:].rearrange("p (i t) -> p i t", i=PACK),
+                in_=rows.rearrange("(p i) t -> p i t", i=PACK),
+            )
+
+        def load_w8(b):
+            words = w8_words[0].rearrange("p j i -> p (j i)")
+            nc.sync.dma_start(out=w8_raw[b][:].bitcast(I32), in_=words[:, 4 * PASS * b : 4 * PASS * (b + 1)].bitcast(I32))
+
+        def load_res(r):
+            nc.sync.dma_start(
+                out=res_sb[r][:], in_=res[:, res_edges[r] : res_edges[r + 1]].rearrange("(g p) t -> p g t", p=P)
+            )
+
+        def order_w8(b):
+            nc.vector.tensor_copy(
+                out=w8[b][:].bitcast(I32).rearrange("p (i c e) -> p c i e", i=PACK, e=4),
+                in_=w8_raw[b][:].bitcast(I32).rearrange("p (c e i) -> p c i e", i=PACK, e=4),
+            )
+
+        def order_w4(b):
+            nc.vector.tensor_copy(
+                out=w4[b][:].rearrange("p (i c m e) -> p c i m e", i=PACK, m=8, e=2),
+                in_=w4_raw[b][:].rearrange("p (c m i e) -> p c i m e", i=PACK, m=8, e=2),
+            )
+
+        def order_w_scales(b):
+            nc.vector.tensor_copy(
+                out=w_sc[:, PASS * b : PASS * (b + 1)].rearrange("p (i c m) -> p c i m", i=PACK, m=16),
+                in_=w_sc_raw[:, PASS * b : PASS * (b + 1)].rearrange("p (c m i) -> p c i m", i=PACK, m=16),
+            )
+
+        def interleave_x(c, a, on_vector):
+            dst = x_bf[c][a][:].rearrange("p (c e i) -> p c i e", i=PACK, e=4)
+            src = x_raw[c][a][:].rearrange("p (i c e) -> p c i e", i=PACK, e=4)
+            groups = WIDTHS[c] // 4
+            cut = groups * SHARE[min(2 * c + a, len(SHARE) - 1)] // 16
+            if on_vector and cut > 0:
+                nc.vector.tensor_copy(out=dst[:, :cut], in_=src[:, :cut])
+            if not on_vector and cut < groups:
+                nc.scalar.copy(out=dst[:, cut:], in_=src[:, cut:])
+
+        def quantize(codes, scales, values):
+            nc.vector.quantize_mx(out=codes[:].bitcast(FP8X4), scales=scales[:], in_=values[:])
+
+        def mixed_product(acc, width, w_fp8, w_fp4, plane, col, codes, scales):
+            nc.tensor.matmul_mx(
+                out=acc,
+                lhsT=w_fp8.bitcast(FP8X4),
+                lhsT_scale=plane[FP8_ROW:P, col : col + P],
+                rhs=codes[0][:].bitcast(FP8X4),
+                rhs_scale=scales[0][:],
+                start=True,
+                stop=False,
+            )
+            step = width if width == 512 else P
+            for t0 in range(0, width, step):
+                nc.tensor.matmul_mx(
+                    out=acc[:, t0 : t0 + step],
+                    lhsT=w_fp4.bitcast(FP4X4),
+                    lhsT_scale=plane[:, col : col + P],
+                    rhs=codes[1][:, t0 : t0 + step].bitcast(FP8X4),
+                    rhs_scale=scales[1][:, t0 : t0 + step],
+                    start=False,
+                    stop=(t0 + step == width),
+                )
+
+        def centres(c, b):
+            width = WIDTHS[c]
+            for i in range(PACK):
+                d = d_psum.tile([P, 512], F32, name="d")
+                mixed_product(
+                    d[:, :width],
+                    width,
+                    w8[b][:, P * i : P * (i + 1)],
+                    w4[b][:, 2 * P * i : 2 * P * (i + 1)],
+                    w_sc,
+                    PASS * b + P * i,
+                    x_q[c],
+                    x_sc[c],
+                )
+                nc.scalar.activation(
+                    out=th[c][b][:, width * i : width * (i + 1)], in_=d[:, :width], func=ACT.Tanh, bias=cb_sb[:, b, i : i + 1]
+                )
+
+        def on_scalar(c, b):
+            return 2 * c + b >= WB and (WBONLY == 2 or b == WBONLY) and 2 * c + b < 2 * chunks - 1
+
+        def weigh_s(c, b):
+            width = WIDTHS[c]
+            if on_scalar(c, b):
+                for i in range(PACK):
+                    nc.scalar.activation(out=h_rows[c][b][:, width * i : width * (i + 1)], in_=th[c][b][:, width * i : width * (i + 1)], func=ACT.Copy, scale=cw_sb[:, b, i : i + 1])
+
+        def weigh(c, b):
+            groups = WIDTHS[c] // 4
+            if on_scalar(c, b):
+                nc.vector.tensor_copy(out=h_bf[c][b][:].rearrange("p (c e i) -> p c i e", i=PACK, e=4), in_=h_rows[c][b][:].rearrange("p (i c e) -> p c i e", i=PACK, e=4))
+                return
+            nc.vector.tensor_tensor(
+                out=h_bf[c][b][:].rearrange("p (c e i) -> p c i e", i=PACK, e=4),
+                in0=th[c][b][:].rearrange("p (i c e) -> p c i e", i=PACK, e=4),
+                in1=cw_sb[:, b, :].unsqueeze(1).unsqueeze(3).to_broadcast([P, groups, PACK, 4]),
+                op=ALU.mult,
+            )
+
+        y = {}
+
+        def outputs(c):
+            width = WIDTHS[c]
+            y[c] = y_psum.tile([P, 2, 256], F32, name="y")
+            for g in range(2):
+                mixed_product(
+                    y[c][:, g, :width],
+                    width,
+                    v8[:, P * g : P * (g + 1)],
+                    v4[:, 2 * P * g : 2 * P * (g + 1)],
+                    v_sc,
+                    P * g,
+                    h_q[c],
+                    h_sc[c],
+                )
+
+        def add_residual(c):
+            r = 0 if c < RES_SPLIT else 1
+            t0 = starts[c] - res_edges[r]
+            nc.vector.tensor_tensor(
+                out=out_sb[c][:], in0=y[c][:, :, : WIDTHS[c]], in1=res_sb[r][:, :, t0 : t0 + WIDTHS[c]], op=ALU.add
+            )
+            nc.sync.dma_start(
+                out=out[:, starts[c] : starts[c + 1]].rearrange("(g p) t -> p g t", p=P), in_=out_sb[c][:]
+            )
+
+        nc.vector.memset(w_sc_raw[:].bitcast(I32), 0)
+        nc.vector.memset(warm_in[:], 0.0)
+        nc.vector.memset(v_sc[:].bitcast(I32), 0)
+        nc.scalar.activation(out=warm_out[:], in_=warm_in[:], func=ACT.Tanh)
+
+        def load_w4(b):
+            nc.sync.dma_start(out=w4_raw[b][:].bitcast(I32), in_=w4_words[0][:, 2 * PASS * b : 2 * PASS * (b + 1)].bitcast(I32))
+
+        small = [lambda: nc.gpsimd.dma_start(out=cb_sb[:], in_=cb.rearrange("(b p i) -> p b i", b=2, i=PACK)),
+                 lambda: nc.gpsimd.dma_start(out=cw_sb[:], in_=cw.rearrange("(b p i) -> p b i", b=2, i=PACK))]
+        small[0]()
+        small[1]()
+        load_x(0, 0)
+        load_w4(0)
+        for q in range(4):
+            load_scales(w_sc_raw, 0, w4_scales, q, nc.sync)
+        load_x(0, 1)
+        load_w8(0)
+        for q in range(4):
+            load_scales(w_sc_raw, FP8_ROW, w8_scales, q, nc.sync)
+        load_w4(1)
+        load_w8(1)
+        for n in range(2, 2 * chunks):
+            load_x(n // 2, n % 2)
+            if 2 <= n < 6:
+                load_scales(v_sc, FP8_ROW, v8_scales, n - 2, nc.sync)
+                load_scales(v_sc, 0, v4_scales, n - 2, nc.sync)
+            if n == 5:
+                nc.sync.dma_start(out=v8[:].bitcast(I32), in_=v8_words[0].rearrange("p n i -> p (n i)").bitcast(I32))
+                nc.sync.dma_start(out=v4[:].bitcast(I32), in_=v4_words[0].bitcast(I32))
+            if n == RESAT:
+                load_res(0)
+        load_res(1)
+
+        def warm_pe(count):
+            if count:
+                idle = y_psum.tile([P, 2, 256], F32, name="y")
+                for k in range(count):
+                    nc.tensor.matmul_mx(
+                        out=idle[:, 0, :],
+                        lhsT=x_q[0][0][:, :P].bitcast(FP8X4),
+                        lhsT_scale=x_sc[0][0][:, :P],
+                        rhs=x_q[0][0][:].bitcast(FP8X4),
+                        rhs_scale=x_sc[0][0][:],
+                        start=True,
+                        stop=True,
+                    )
+
+        def quantize_x(n):
+            if n < 2 * chunks:
+                quantize(x_q[n // 2][n % 2], x_sc[n // 2][n % 2], x_bf[n // 2][n % 2])
+
+        def quantize_h(n):
+            quantize(h_q[n // 2][n % 2], h_sc[n // 2][n % 2], h_bf[n // 2][n % 2])
+
+        def ix(n, v):
+            if n < 2 * chunks:
+                interleave_x(n // 2, n % 2, v)
+
+        ix(0, False)
+        ix(0, True)
+        order_w4(0)
+        quantize_x(0)
+        warm_pe(WARM0)
+        ix(1, False)
+        ix(1, True)
+        order_w_scales(0)
+        quantize_x(1)
+        order_w8(0)
+        order_w_scales(1)
+        order_w4(1)
+        order_w8(1)
+
+        steps = [(c, b) for c in range(chunks) for b in range(2)]
+        added = 0
+        made = 0
+        for n, (c, b) in enumerate(steps):
+            last = n == len(steps) - 1
+            pieces = [n + 2] if n < N1 else [n + 2, n + 3] if n == N1 else [n + 3] if n < N0 else [n + 3, n + 4] if n == N0 else [n + 4]
+            centres(c, b)
+            weigh_s(c, b)
+            if 2 * made + 3 + OL <= n:
+                outputs(made)
+                made += 1
+            for m in pieces:
+                ix(m, False)
+            if n < PRE:
+                for m in pieces:
+                    ix(m, True)
+                    quantize_x(m)
+            weigh(c, b)
+            if n >= PRE:
+                for m in pieces:
+                    ix(m, True)
+            if n > 0:
+                quantize_h(n - 1)
+            if n >= PRE:
+                for m in pieces:
+                    quantize_x(m)
+            if n >= ADD0 and added < made and not last:
+                add_residual(added)
+                added += 1
+        quantize_h(2 * chunks - 1)
+        while made < chunks:
+            if added < made - 1:
+                add_residual(added)
+                added += 1
+            outputs(made)
+            made += 1
+        while added < chunks:
+            add_residual(added)
+            added += 1

@@ -23,23 +23,25 @@ WIDTHS = [256,256,256,128,128]
 RES_SPLIT = 1
 XV = 4
 SPLIT = 4
-WB = 99
-WBONLY = 1
+WB = 7
+WBONLY = 0
 ORDER = 1
 GS = 0
 RESAT = 9
 EARLY = 1
-N0 = 4
+E = 2
+N0 = 3
 N1 = 0
 PRE = 3
-SHARE = [4, 8, 16, 16, 4, 4, 0]
+SHARE = [4, 8, 16, 16, 5, 5, 0]
 S3 = 6
 WARM0 = 6
-WARM1 = 4
+WARM1 = 0
+WARM3 = 0
 XV0 = 2
 XS = 8
 OL = 1
-ADD0 = 4
+ADD0 = 5
 
 
 def tile_mix_kern_outl_tanh_mix_res_kernel(
@@ -130,9 +132,9 @@ def tile_mix_kern_outl_tanh_mix_res_kernel(
             )
 
         def interleave_x(c, a, on_vector):
-            dst = x_bf[c][a][:].rearrange("p (c e i) -> p c i e", i=PACK, e=4)
-            src = x_raw[c][a][:].rearrange("p (i c e) -> p c i e", i=PACK, e=4)
-            groups = WIDTHS[c] // 4
+            dst = x_bf[c][a][:].rearrange("p (c e i) -> p c i e", i=PACK, e=E)
+            src = x_raw[c][a][:].rearrange("p (i c e) -> p c i e", i=PACK, e=E)
+            groups = WIDTHS[c] // E
             cut = groups * SHARE[min(2 * c + a, len(SHARE) - 1)] // 16
             if on_vector and cut > 0:
                 nc.vector.tensor_copy(out=dst[:, :cut], in_=src[:, :cut])
@@ -192,14 +194,13 @@ def tile_mix_kern_outl_tanh_mix_res_kernel(
                     nc.scalar.activation(out=h_rows[c][b][:, width * i : width * (i + 1)], in_=th[c][b][:, width * i : width * (i + 1)], func=ACT.Copy, scale=cw_sb[:, b, i : i + 1])
 
         def weigh(c, b):
-            groups = WIDTHS[c] // 4
             if on_scalar(c, b):
                 nc.vector.tensor_copy(out=h_bf[c][b][:].rearrange("p (c e i) -> p c i e", i=PACK, e=4), in_=h_rows[c][b][:].rearrange("p (i c e) -> p c i e", i=PACK, e=4))
                 return
             nc.vector.tensor_tensor(
-                out=h_bf[c][b][:].rearrange("p (c e i) -> p c i e", i=PACK, e=4),
-                in0=th[c][b][:].rearrange("p (i c e) -> p c i e", i=PACK, e=4),
-                in1=cw_sb[:, b, :].unsqueeze(1).unsqueeze(3).to_broadcast([P, groups, PACK, 4]),
+                out=h_bf[c][b][:].rearrange("p (c e i) -> p c i e", i=PACK, e=E),
+                in0=th[c][b][:].rearrange("p (i c e) -> p c i e", i=PACK, e=E),
+                in1=cw_sb[:, b, :].unsqueeze(1).unsqueeze(3).to_broadcast([P, WIDTHS[c] // E, PACK, E]),
                 op=ALU.mult,
             )
 
@@ -238,20 +239,20 @@ def tile_mix_kern_outl_tanh_mix_res_kernel(
         def load_w4(b):
             nc.sync.dma_start(out=w4_raw[b][:].bitcast(I32), in_=w4_words[0][:, 2 * PASS * b : 2 * PASS * (b + 1)].bitcast(I32))
 
-        small = [lambda: nc.gpsimd.dma_start(out=cb_sb[:], in_=cb.rearrange("(b p i) -> p b i", b=2, i=PACK)),
-                 lambda: nc.gpsimd.dma_start(out=cw_sb[:], in_=cw.rearrange("(b p i) -> p b i", b=2, i=PACK))]
-        small[0]()
-        small[1]()
+        small = [lambda: nc.sync.dma_start(out=cb_sb[:], in_=cb.rearrange("(b p i) -> p b i", b=2, i=PACK)),
+                 lambda: nc.sync.dma_start(out=cw_sb[:], in_=cw.rearrange("(b p i) -> p b i", b=2, i=PACK))]
         load_x(0, 0)
         load_w4(0)
         for q in range(4):
             load_scales(w_sc_raw, 0, w4_scales, q, nc.sync)
+        for q in range(4):
+            load_scales(w_sc_raw, FP8_ROW, w8_scales, q, nc.gpsimd if q < 3 else nc.sync)
         load_x(0, 1)
         load_w8(0)
-        for q in range(4):
-            load_scales(w_sc_raw, FP8_ROW, w8_scales, q, nc.sync)
+        small[0]()
         load_w4(1)
         load_w8(1)
+        small[1]()
         for n in range(2, 2 * chunks):
             load_x(n // 2, n % 2)
             if 2 <= n < 6:
@@ -297,8 +298,8 @@ def tile_mix_kern_outl_tanh_mix_res_kernel(
         ix(1, False)
         ix(1, True)
         order_w_scales(0)
-        quantize_x(1)
         order_w8(0)
+        quantize_x(1)
         order_w_scales(1)
         order_w4(1)
         order_w8(1)
@@ -310,6 +311,10 @@ def tile_mix_kern_outl_tanh_mix_res_kernel(
             last = n == len(steps) - 1
             pieces = [n + 2] if n < N1 else [n + 2, n + 3] if n == N1 else [n + 3] if n < N0 else [n + 3, n + 4] if n == N0 else [n + 4]
             centres(c, b)
+            if n == 1:
+                warm_pe(WARM1)
+            if n == 3:
+                warm_pe(WARM3)
             weigh_s(c, b)
             if 2 * made + 3 + OL <= n:
                 outputs(made)

@@ -1,6 +1,7 @@
 from contextlib import ExitStack
 
 import concourse.mybir as mybir
+from concourse.masks import make_identity
 
 K, J, N, T = 1024, 1024, 256, 1024
 FLOPS = 2 * K * J * T + 2 * J * N * T
@@ -23,24 +24,33 @@ WIDTHS = [256,256,256,128,128]
 RES_SPLIT = 1
 XV = 4
 SPLIT = 4
-WB = 7
-WBONLY = 0
+WB = 5
+WBONLY = 1
 ORDER = 1
-GS = 0
+GS = 3
 RESAT = 9
 EARLY = 1
 E = 2
+G0 = 4
+GMAX = 128
+LATE = 10
+G1 = 10
+LASTAT = 4
+GSHARE = [0, 0, 0, 0, 0, 0, 16]
+GSTEP = 128
+PACKB = 1
+QF = 0
 N0 = 3
 N1 = 0
-PRE = 3
-SHARE = [4, 8, 16, 16, 5, 5, 0]
+PRE = 1
+SHARE = [4, 8, 16, 16, 0, 0, 0]
 S3 = 6
 WARM0 = 6
 WARM1 = 0
 WARM3 = 0
 XV0 = 2
 XS = 8
-OL = 1
+OL = 2
 ADD0 = 5
 
 
@@ -53,8 +63,9 @@ def tile_mix_kern_outl_tanh_mix_res_kernel(
 
     with ExitStack() as ctx:
         sb = ctx.enter_context(tc.tile_pool(name="sb", bufs=1))
-        d_psum = ctx.enter_context(tc.psum_pool(name="d_psum", bufs=6))
+        d_psum = ctx.enter_context(tc.psum_pool(name="d_psum", bufs=5))
         y_psum = ctx.enter_context(tc.psum_pool(name="y_psum", bufs=2))
+        c_psum = ctx.enter_context(tc.psum_pool(name="c_psum", bufs=1))
         ctx.enter_context(tc.manual_schedule())
 
         def keep(name, shape, dtype):
@@ -70,7 +81,11 @@ def tile_mix_kern_outl_tanh_mix_res_kernel(
         v4 = keep("v4", [P, 2 * N], U8)
         v_sc = keep("v_sc", [P, N], U8)
         cb_sb = keep("cb_sb", [P, 2, PACK], F32)
-        cw_sb = keep("cw_sb", [P, 2, PACK], F32)
+        cw_pad = keep("cw_pad", [P, P], F32)
+        cw_sb = cw_pad[:, : 2 * PACK].rearrange("p (b i) -> p b i", b=2)
+        cw_rows = keep("cw_rows", [P, P], F32)
+        ident = keep("ident", [P, P], F32)
+        cw_ps = c_psum.tile([P, P], F32, name="cw_ps")
         warm_in = keep("warm_in", [P, 1], F32)
         warm_out = keep("warm_out", [P, 1], F32)
 
@@ -78,7 +93,7 @@ def tile_mix_kern_outl_tanh_mix_res_kernel(
             return [[keep("%s%d_%d" % (name, c, a), [P, cols * WIDTHS[c]], dtype) for a in range(2)] for c in range(chunks)]
 
         x_raw = per_half("x_raw", PACK, F32)
-        x_bf = per_half("x_bf", PACK, BF16)
+        x_bf = {}
         x_q = per_half("x_q", 1, U32)
         x_sc = per_half("x_sc", 1, U8)
         th = per_half("th", PACK, F32)
@@ -132,14 +147,22 @@ def tile_mix_kern_outl_tanh_mix_res_kernel(
             )
 
         def interleave_x(c, a, on_vector):
-            dst = x_bf[c][a][:].rearrange("p (c e i) -> p c i e", i=PACK, e=E)
+            if (c, a) not in x_bf:
+                tag = "x_bf_late" if G0 - 1 <= 2 * c + a < G1 else "x_bf%d_%d" % (c, a)
+                x_bf[c, a] = sb.tile([P, PACK * WIDTHS[c]], BF16, name="x_bf%d_%d" % (c, a), tag=tag, align_bytes=64)
+            dst = x_bf[c, a][:].rearrange("p (c e i) -> p c i e", i=PACK, e=E)
             src = x_raw[c][a][:].rearrange("p (i c e) -> p c i e", i=PACK, e=E)
             groups = WIDTHS[c] // E
             cut = groups * SHARE[min(2 * c + a, len(SHARE) - 1)] // 16
-            if on_vector and cut > 0:
+            top = max(0, groups - GMAX // E) if G0 <= 2 * c + a < G1 else groups
+            if on_vector == 1 and cut > 0:
                 nc.vector.tensor_copy(out=dst[:, :cut], in_=src[:, :cut])
-            if not on_vector and cut < groups:
-                nc.scalar.copy(out=dst[:, cut:], in_=src[:, cut:])
+            if on_vector == 0 and cut < top:
+                nc.scalar.copy(out=dst[:, cut:top], in_=src[:, cut:top])
+            if on_vector == 2:
+                for g0 in range(top, groups, GSTEP):
+                    g1 = min(groups, g0 + GSTEP)
+                    nc.gpsimd.tensor_scalar(out=dst[:, g0:g1], in0=src[:, g0:g1], scalar1=1.0, scalar2=0.0, op0=ALU.mult, op1=ALU.add)
 
         def quantize(codes, scales, values):
             nc.vector.quantize_mx(out=codes[:].bitcast(FP8X4), scales=scales[:], in_=values[:])
@@ -168,10 +191,13 @@ def tile_mix_kern_outl_tanh_mix_res_kernel(
 
         def centres(c, b):
             width = WIDTHS[c]
+            per_bank = PACKB if width == P else 1
             for i in range(PACK):
-                d = d_psum.tile([P, 512], F32, name="d")
+                if i % per_bank == 0:
+                    bank = d_psum.tile([P, 512], F32, name="d")
+                d = bank[:, (i % per_bank) * width : (i % per_bank + 1) * width]
                 mixed_product(
-                    d[:, :width],
+                    d,
                     width,
                     w8[b][:, P * i : P * (i + 1)],
                     w4[b][:, 2 * P * i : 2 * P * (i + 1)],
@@ -180,9 +206,14 @@ def tile_mix_kern_outl_tanh_mix_res_kernel(
                     x_q[c],
                     x_sc[c],
                 )
-                nc.scalar.activation(
-                    out=th[c][b][:, width * i : width * (i + 1)], in_=d[:, :width], func=ACT.Tanh, bias=cb_sb[:, b, i : i + 1]
-                )
+                if i % per_bank == per_bank - 1:
+                    for k in range(i + 1 - per_bank, i + 1):
+                        nc.scalar.activation(
+                            out=th[c][b][:, width * k : width * (k + 1)],
+                            in_=bank[:, (k % per_bank) * width : (k % per_bank + 1) * width],
+                            func=ACT.Tanh,
+                            bias=cb_sb[:, b, k : k + 1],
+                        )
 
         def on_scalar(c, b):
             return 2 * c + b >= WB and (WBONLY == 2 or b == WBONLY) and 2 * c + b < 2 * chunks - 1
@@ -200,7 +231,7 @@ def tile_mix_kern_outl_tanh_mix_res_kernel(
             nc.vector.tensor_tensor(
                 out=h_bf[c][b][:].rearrange("p (c e i) -> p c i e", i=PACK, e=E),
                 in0=th[c][b][:].rearrange("p (i c e) -> p c i e", i=PACK, e=E),
-                in1=cw_sb[:, b, :].unsqueeze(1).unsqueeze(3).to_broadcast([P, WIDTHS[c] // E, PACK, E]),
+                in1=cw_ps[:, PACK * b : PACK * (b + 1)].unsqueeze(1).unsqueeze(3).to_broadcast([P, WIDTHS[c] // E, PACK, E]),
                 op=ALU.mult,
             )
 
@@ -234,25 +265,27 @@ def tile_mix_kern_outl_tanh_mix_res_kernel(
         nc.vector.memset(w_sc_raw[:].bitcast(I32), 0)
         nc.vector.memset(warm_in[:], 0.0)
         nc.vector.memset(v_sc[:].bitcast(I32), 0)
+        nc.vector.memset(cw_pad[:], 0.0)
         nc.scalar.activation(out=warm_out[:], in_=warm_in[:], func=ACT.Tanh)
 
         def load_w4(b):
             nc.sync.dma_start(out=w4_raw[b][:].bitcast(I32), in_=w4_words[0][:, 2 * PASS * b : 2 * PASS * (b + 1)].bitcast(I32))
 
         small = [lambda: nc.sync.dma_start(out=cb_sb[:], in_=cb.rearrange("(b p i) -> p b i", b=2, i=PACK)),
-                 lambda: nc.sync.dma_start(out=cw_sb[:], in_=cw.rearrange("(b p i) -> p b i", b=2, i=PACK))]
+                 lambda: nc.sync.dma_start(out=cw_sb, in_=cw.rearrange("(b p i) -> p b i", b=2, i=PACK))]
         load_x(0, 0)
         load_w4(0)
         for q in range(4):
             load_scales(w_sc_raw, 0, w4_scales, q, nc.sync)
         for q in range(4):
-            load_scales(w_sc_raw, FP8_ROW, w8_scales, q, nc.gpsimd if q < 3 else nc.sync)
+            load_scales(w_sc_raw, FP8_ROW, w8_scales, q, nc.gpsimd if q < GS else nc.sync)
+        make_identity(nc, ident[:])
         load_x(0, 1)
         load_w8(0)
         small[0]()
+        small[1]()
         load_w4(1)
         load_w8(1)
-        small[1]()
         for n in range(2, 2 * chunks):
             load_x(n // 2, n % 2)
             if 2 <= n < 6:
@@ -281,7 +314,7 @@ def tile_mix_kern_outl_tanh_mix_res_kernel(
 
         def quantize_x(n):
             if n < 2 * chunks:
-                quantize(x_q[n // 2][n % 2], x_sc[n // 2][n % 2], x_bf[n // 2][n % 2])
+                quantize(x_q[n // 2][n % 2], x_sc[n // 2][n % 2], x_bf[n // 2, n % 2])
 
         def quantize_h(n):
             quantize(h_q[n // 2][n % 2], h_sc[n // 2][n % 2], h_bf[n // 2][n % 2])
@@ -309,34 +342,54 @@ def tile_mix_kern_outl_tanh_mix_res_kernel(
         made = 0
         for n, (c, b) in enumerate(steps):
             last = n == len(steps) - 1
-            pieces = [n + 2] if n < N1 else [n + 2, n + 3] if n == N1 else [n + 3] if n < N0 else [n + 3, n + 4] if n == N0 else [n + 4]
-            centres(c, b)
-            if n == 1:
-                warm_pe(WARM1)
-            if n == 3:
-                warm_pe(WARM3)
+            pieces = [2, 3] if n == 0 else [n + 3]
+            if n != 1:
+                centres(c, b)
+            if n == 0:
+                there = y_psum.tile([P, 2, 256], F32, name="y")
+                nc.tensor.transpose(there[:, 0, :P], cw_pad[:], ident[:])
+                nc.scalar.copy(out=cw_rows[:], in_=there[:, 0, :P])
+            if n == LASTAT:
+                for m in range(G1, 2 * chunks):
+                    ix(m, False)
             weigh_s(c, b)
             if 2 * made + 3 + OL <= n:
                 outputs(made)
                 made += 1
-            for m in pieces:
-                ix(m, False)
+            if n == 0:
+                centres(0, 1)
+                nc.tensor.transpose(cw_ps[:], cw_rows[:], ident[:])
             if n < PRE:
                 for m in pieces:
-                    ix(m, True)
-                    quantize_x(m)
-            weigh(c, b)
-            if n >= PRE:
+                    ix(m, False)
+                if n > 1:
+                    quantize_h(n - 2)
                 for m in pieces:
                     ix(m, True)
-            if n > 0:
-                quantize_h(n - 1)
-            if n >= PRE:
-                for m in pieces:
                     quantize_x(m)
-            if n >= ADD0 and added < made and not last:
-                add_residual(added)
-                added += 1
+                if n + 4 >= G0:
+                    ix(n + 4, 2)
+                weigh(c, b)
+            else:
+                if n + 3 < G1:
+                    ix(n + 3, 0)
+                if n > 1:
+                    quantize_h(n - 2)
+                if n == LASTAT + 1:
+                    for m in range(G1, 2 * chunks):
+                        quantize_x(m)
+                if n + 3 < G1:
+                    quantize_x(n + 3)
+                if n + 4 < G1:
+                    ix(n + 4, 2)
+                if n >= LATE and added < made:
+                    add_residual(added)
+                    added += 1
+                weigh(c, b)
+                if ADD0 <= n < LATE and added < made:
+                    add_residual(added)
+                    added += 1
+        quantize_h(2 * chunks - 2)
         quantize_h(2 * chunks - 1)
         while made < chunks:
             if added < made - 1:

@@ -18,385 +18,334 @@ ALU = mybir.AluOpType
 
 P = 128
 PACK = 4
-PASS = P * PACK
+HALF = P * PACK
+BANK = 512
+QUADS = 4
 FP8_ROW = 4
-WIDTHS = [256,256,256,128,128]
-RES_SPLIT = 1
-XV = 4
-SPLIT = 4
-WB = 5
-WBONLY = 1
-ORDER = 1
-GS = 3
-RESAT = 9
-EARLY = 1
-E = 2
-G0 = 4
-GMAX = 128
-LATE = 10
-G1 = 10
-LASTAT = 4
-GSHARE = [0, 0, 0, 0, 0, 0, 16]
-GSTEP = 128
-PACKB = 1
-QF = 0
-N0 = 3
-N1 = 0
-PRE = 1
-SHARE = [4, 8, 16, 16, 0, 0, 0]
-S3 = 6
-WARM0 = 6
-WARM1 = 0
-WARM3 = 0
-XV0 = 2
-XS = 8
-OL = 2
-ADD0 = 5
+PAIR = 2
+
+WIDTHS = [256, 256, 256, 128, 128]
+CHUNKS = len(WIDTHS)
+STEPS = 2 * CHUNKS
+STARTS = [sum(WIDTHS[:c]) for c in range(CHUNKS + 1)]
+VECTOR_COLS = [64, 128]
+GPSIMD_COLS = 128
+FIRST_GPSIMD_PIECE = 4
+SCALAR_WEIGHS = range(FIRST_GPSIMD_PIECE + 1, STEPS - 1, 2)
+GPSIMD_SCALE_LOADS = 3
+WARM_PASSES = 6
 
 
 def tile_mix_kern_outl_tanh_mix_res_kernel(
     tc, x, w8_words, w8_scales, w4_words, w4_scales, cw, cb, v8_words, v8_scales, v4_words, v4_scales, res, out
 ):
     nc = tc.nc
-    chunks = len(WIDTHS)
-    starts = [sum(WIDTHS[:c]) for c in range(chunks + 1)]
 
     with ExitStack() as ctx:
         sb = ctx.enter_context(tc.tile_pool(name="sb", bufs=1))
         d_psum = ctx.enter_context(tc.psum_pool(name="d_psum", bufs=5))
         y_psum = ctx.enter_context(tc.psum_pool(name="y_psum", bufs=2))
-        c_psum = ctx.enter_context(tc.psum_pool(name="c_psum", bufs=1))
+        cw_psum = ctx.enter_context(tc.psum_pool(name="cw_psum", bufs=1))
         ctx.enter_context(tc.manual_schedule())
 
         def keep(name, shape, dtype):
             return sb.tile(shape, dtype, name=name, align_bytes=64)
 
-        w8_raw = [keep("w8_raw%d" % b, [P, PASS], U32) for b in range(2)]
-        w8 = [keep("w8_%d" % b, [P, PASS], U32) for b in range(2)]
-        w4_raw = [keep("w4_raw%d" % b, [P, 2 * PASS], U8) for b in range(2)]
-        w4 = [keep("w4_%d" % b, [P, 2 * PASS], U8) for b in range(2)]
+        def per_step(name, cols, dtype, steps):
+            return {n: keep("%s%d" % (name, n), [P, cols * WIDTHS[n // 2]], dtype) for n in steps}
+
+        w8_raw = [keep("w8_raw%d" % b, [P, HALF], U32) for b in range(2)]
+        w8 = [keep("w8_%d" % b, [P, HALF], U32) for b in range(2)]
+        w4_raw = [keep("w4_raw%d" % b, [P, 2 * HALF], U8) for b in range(2)]
+        w4 = [keep("w4_%d" % b, [P, 2 * HALF], U8) for b in range(2)]
         w_sc_raw = keep("w_sc_raw", [P, J], U8)
         w_sc = keep("w_sc", [P, J], U8)
         v8 = keep("v8", [P, N], U32)
         v4 = keep("v4", [P, 2 * N], U8)
         v_sc = keep("v_sc", [P, N], U8)
         cb_sb = keep("cb_sb", [P, 2, PACK], F32)
-        cw_pad = keep("cw_pad", [P, P], F32)
-        cw_sb = cw_pad[:, : 2 * PACK].rearrange("p (b i) -> p b i", b=2)
-        cw_rows = keep("cw_rows", [P, P], F32)
+        cw_square = keep("cw_square", [P, P], F32)
+        cw_sb = cw_square[:, : 2 * PACK].rearrange("p (b i) -> p b i", b=2)
+        cw_turned = keep("cw_turned", [P, P], F32)
         ident = keep("ident", [P, P], F32)
-        cw_ps = c_psum.tile([P, P], F32, name="cw_ps")
+        cw_ps = cw_psum.tile([P, P], F32, name="cw_ps")
         warm_in = keep("warm_in", [P, 1], F32)
         warm_out = keep("warm_out", [P, 1], F32)
 
-        def per_half(name, cols, dtype):
-            return [[keep("%s%d_%d" % (name, c, a), [P, cols * WIDTHS[c]], dtype) for a in range(2)] for c in range(chunks)]
-
-        x_raw = per_half("x_raw", PACK, F32)
+        x_raw = per_step("x_raw", PACK, F32, range(STEPS))
         x_bf = {}
-        x_q = per_half("x_q", 1, U32)
-        x_sc = per_half("x_sc", 1, U8)
-        th = per_half("th", PACK, F32)
-        h_bf = per_half("h_bf", PACK, BF16)
-        h_rows = per_half("h_rows", PACK, BF16)
-        h_q = per_half("h_q", 1, U32)
-        h_sc = per_half("h_sc", 1, U8)
-        res_edges = [0, starts[RES_SPLIT], T]
+        x_q = per_step("x_q", 1, U32, range(STEPS - 2))
+        x_sc = per_step("x_sc", 1, U8, range(STEPS - 2))
+        x_q_last = keep("x_q_last", [P, 2 * WIDTHS[-1]], U32)
+        x_sc_last = keep("x_sc_last", [P, 2 * WIDTHS[-1]], U8)
+        for a in range(2):
+            x_q[STEPS - 2 + a] = x_q_last[:, a * WIDTHS[-1] : (a + 1) * WIDTHS[-1]]
+            x_sc[STEPS - 2 + a] = x_sc_last[:, a * WIDTHS[-1] : (a + 1) * WIDTHS[-1]]
+        tanh_d = per_step("tanh_d", PACK, F32, range(STEPS))
+        h_rows = per_step("h_rows", PACK, BF16, SCALAR_WEIGHS)
+        h_bf = per_step("h_bf", PACK, BF16, range(STEPS))
+        h_q = per_step("h_q", 1, U32, range(STEPS))
+        h_sc = per_step("h_sc", 1, U8, range(STEPS))
+        res_edges = [0, STARTS[1], T]
         res_sb = [keep("res%d" % r, [P, 2, res_edges[r + 1] - res_edges[r]], F32) for r in range(2)]
-        out_sb = [keep("out%d" % c, [P, 2, WIDTHS[c]], F32) for c in range(chunks)]
+        out_sb = [keep("out%d" % c, [P, 2, WIDTHS[c]], F32) for c in range(CHUNKS)]
+        y = {}
 
-        def load_scales(plane, row, scales, q, queue):
-            if True:
-                queue.dma_start(
-                    out=plane[32 * q + row : 32 * q + row + 4, :].bitcast(I32),
-                    in_=scales[0, 4 * q : 4 * q + 4, :].bitcast(I32),
-                )
+        def load_scales(queue, tile, row, scales, quad):
+            queue.dma_start(
+                out=tile[32 * quad + row : 32 * quad + row + 4, :].bitcast(I32),
+                in_=scales[0, 4 * quad : 4 * quad + 4, :].bitcast(I32),
+            )
 
-        def load_x(c, a):
-            rows = x[a * PASS : (a + 1) * PASS, starts[c] : starts[c + 1]]
+        def load_x(n):
+            c, a = divmod(n, 2)
+            rows = x[a * HALF : (a + 1) * HALF, STARTS[c] : STARTS[c + 1]]
             nc.sync.dma_start(
-                out=x_raw[c][a][:].rearrange("p (i t) -> p i t", i=PACK),
+                out=x_raw[n][:].rearrange("p (i t) -> p i t", i=PACK),
                 in_=rows.rearrange("(p i) t -> p i t", i=PACK),
             )
 
         def load_w8(b):
             words = w8_words[0].rearrange("p j i -> p (j i)")
-            nc.sync.dma_start(out=w8_raw[b][:].bitcast(I32), in_=words[:, 4 * PASS * b : 4 * PASS * (b + 1)].bitcast(I32))
+            nc.sync.dma_start(out=w8_raw[b][:].bitcast(I32), in_=words[:, 4 * HALF * b : 4 * HALF * (b + 1)].bitcast(I32))
 
-        def load_res(r):
+        def load_w4(b):
             nc.sync.dma_start(
-                out=res_sb[r][:], in_=res[:, res_edges[r] : res_edges[r + 1]].rearrange("(g p) t -> p g t", p=P)
+                out=w4_raw[b][:].bitcast(I32), in_=w4_words[0][:, 2 * HALF * b : 2 * HALF * (b + 1)].bitcast(I32)
             )
 
-        def order_w8(b):
+        def gather_w8(b):
             nc.vector.tensor_copy(
-                out=w8[b][:].bitcast(I32).rearrange("p (i c e) -> p c i e", i=PACK, e=4),
-                in_=w8_raw[b][:].bitcast(I32).rearrange("p (c e i) -> p c i e", i=PACK, e=4),
+                out=w8[b][:].bitcast(I32).rearrange("p (i r m) -> p r i m", i=PACK, m=4),
+                in_=w8_raw[b][:].bitcast(I32).rearrange("p (r m i) -> p r i m", i=PACK, m=4),
             )
 
-        def order_w4(b):
+        def gather_w4(b):
             nc.vector.tensor_copy(
-                out=w4[b][:].rearrange("p (i c m e) -> p c i m e", i=PACK, m=8, e=2),
-                in_=w4_raw[b][:].rearrange("p (c m i e) -> p c i m e", i=PACK, m=8, e=2),
+                out=w4[b][:].rearrange("p (i r m byte) -> p r i m byte", i=PACK, m=8, byte=2),
+                in_=w4_raw[b][:].rearrange("p (r m i byte) -> p r i m byte", i=PACK, m=8, byte=2),
             )
 
-        def order_w_scales(b):
+        def gather_w_scales(b):
+            cols = slice(HALF * b, HALF * (b + 1))
             nc.vector.tensor_copy(
-                out=w_sc[:, PASS * b : PASS * (b + 1)].rearrange("p (i c m) -> p c i m", i=PACK, m=16),
-                in_=w_sc_raw[:, PASS * b : PASS * (b + 1)].rearrange("p (c m i) -> p c i m", i=PACK, m=16),
+                out=w_sc[:, cols].rearrange("p (i r m) -> p r i m", i=PACK, m=16),
+                in_=w_sc_raw[:, cols].rearrange("p (r m i) -> p r i m", i=PACK, m=16),
             )
 
-        def interleave_x(c, a, on_vector):
-            if (c, a) not in x_bf:
-                tag = "x_bf_late" if G0 - 1 <= 2 * c + a < G1 else "x_bf%d_%d" % (c, a)
-                x_bf[c, a] = sb.tile([P, PACK * WIDTHS[c]], BF16, name="x_bf%d_%d" % (c, a), tag=tag, align_bytes=64)
-            dst = x_bf[c, a][:].rearrange("p (c e i) -> p c i e", i=PACK, e=E)
-            src = x_raw[c][a][:].rearrange("p (i c e) -> p c i e", i=PACK, e=E)
-            groups = WIDTHS[c] // E
-            cut = groups * SHARE[min(2 * c + a, len(SHARE) - 1)] // 16
-            top = max(0, groups - GMAX // E) if G0 <= 2 * c + a < G1 else groups
-            if on_vector == 1 and cut > 0:
-                nc.vector.tensor_copy(out=dst[:, :cut], in_=src[:, :cut])
-            if on_vector == 0 and cut < top:
-                nc.scalar.copy(out=dst[:, cut:top], in_=src[:, cut:top])
-            if on_vector == 2:
-                for g0 in range(top, groups, GSTEP):
-                    g1 = min(groups, g0 + GSTEP)
-                    nc.gpsimd.tensor_scalar(out=dst[:, g0:g1], in0=src[:, g0:g1], scalar1=1.0, scalar2=0.0, op0=ALU.mult, op1=ALU.add)
+        def words_of(tile):
+            return tile.rearrange("p (r e i) -> p r i e", i=PACK, e=PAIR)
+
+        def rows_of(tile):
+            return tile.rearrange("p (i r e) -> p r i e", i=PACK, e=PAIR)
+
+        def stage(n, shared):
+            tag = "x_bf_shared" if shared else "x_bf%d" % n
+            pieces = 2 if n == STEPS - 2 else 1
+            cols = PACK * WIDTHS[n // 2]
+            whole = sb.tile([P, pieces * cols], BF16, name="x_bf%d" % n, tag=tag, align_bytes=64)
+            x_bf["whole", n] = whole
+            for a in range(pieces):
+                x_bf[n + a] = whole[:, a * cols : (a + 1) * cols]
+
+        def interleave(engine, n, t0, t1):
+            dst = words_of(x_bf[n])[:, t0 // PAIR : t1 // PAIR]
+            src = rows_of(x_raw[n][:])[:, t0 // PAIR : t1 // PAIR]
+            if engine == "vector":
+                nc.vector.tensor_copy(out=dst, in_=src)
+            elif engine == "scalar":
+                nc.scalar.copy(out=dst, in_=src)
+            else:
+                nc.gpsimd.tensor_scalar(out=dst, in0=src, scalar1=1.0, scalar2=0.0, op0=ALU.mult, op1=ALU.add)
 
         def quantize(codes, scales, values):
             nc.vector.quantize_mx(out=codes[:].bitcast(FP8X4), scales=scales[:], in_=values[:])
 
-        def mixed_product(acc, width, w_fp8, w_fp4, plane, col, codes, scales):
+        def quantize_x(n):
+            if n == STEPS - 2:
+                quantize(x_q_last, x_sc_last, x_bf["whole", n])
+            else:
+                quantize(x_q[n], x_sc[n], x_bf["whole", n])
+
+        def quantize_h(n):
+            quantize(h_q[n], h_sc[n], h_bf[n])
+
+        def fp8_pass(acc, weights, w_scales, codes, scales, start):
             nc.tensor.matmul_mx(
                 out=acc,
-                lhsT=w_fp8.bitcast(FP8X4),
-                lhsT_scale=plane[FP8_ROW:P, col : col + P],
-                rhs=codes[0][:].bitcast(FP8X4),
-                rhs_scale=scales[0][:],
-                start=True,
+                lhsT=weights.bitcast(FP8X4),
+                lhsT_scale=w_scales[FP8_ROW:P, :],
+                rhs=codes[:].bitcast(FP8X4),
+                rhs_scale=scales[:],
+                start=start,
                 stop=False,
             )
-            step = width if width == 512 else P
-            for t0 in range(0, width, step):
+
+        def fp4_passes(acc, width, weights, w_scales, codes, scales, stop):
+            for t0 in range(0, width, P):
                 nc.tensor.matmul_mx(
-                    out=acc[:, t0 : t0 + step],
-                    lhsT=w_fp4.bitcast(FP4X4),
-                    lhsT_scale=plane[:, col : col + P],
-                    rhs=codes[1][:, t0 : t0 + step].bitcast(FP8X4),
-                    rhs_scale=scales[1][:, t0 : t0 + step],
+                    out=acc[:, t0 : t0 + P],
+                    lhsT=weights.bitcast(FP4X4),
+                    lhsT_scale=w_scales,
+                    rhs=codes[:, t0 : t0 + P].bitcast(FP8X4),
+                    rhs_scale=scales[:, t0 : t0 + P],
                     start=False,
-                    stop=(t0 + step == width),
+                    stop=stop and t0 + P == width,
                 )
 
-        def centres(c, b):
+        def centres(n):
+            c, b = divmod(n, 2)
             width = WIDTHS[c]
-            per_bank = PACKB if width == P else 1
             for i in range(PACK):
-                if i % per_bank == 0:
-                    bank = d_psum.tile([P, 512], F32, name="d")
-                d = bank[:, (i % per_bank) * width : (i % per_bank + 1) * width]
-                mixed_product(
-                    d,
-                    width,
-                    w8[b][:, P * i : P * (i + 1)],
-                    w4[b][:, 2 * P * i : 2 * P * (i + 1)],
-                    w_sc,
-                    PASS * b + P * i,
-                    x_q[c],
-                    x_sc[c],
+                bank = d_psum.tile([P, BANK], F32, name="d")
+                d = bank[:, :width]
+                w_scales = w_sc[:, HALF * b + P * i : HALF * b + P * (i + 1)]
+                fp8_pass(d, w8[b][:, P * i : P * (i + 1)], w_scales, x_q[2 * c], x_sc[2 * c], True)
+                fp4_passes(d, width, w4[b][:, 2 * P * i : 2 * P * (i + 1)], w_scales, x_q[2 * c + 1], x_sc[2 * c + 1], True)
+                nc.scalar.activation(
+                    out=tanh_d[n][:, width * i : width * (i + 1)], in_=d, func=ACT.Tanh, bias=cb_sb[:, b, i : i + 1]
                 )
-                if i % per_bank == per_bank - 1:
-                    for k in range(i + 1 - per_bank, i + 1):
-                        nc.scalar.activation(
-                            out=th[c][b][:, width * k : width * (k + 1)],
-                            in_=bank[:, (k % per_bank) * width : (k % per_bank + 1) * width],
-                            func=ACT.Tanh,
-                            bias=cb_sb[:, b, k : k + 1],
-                        )
 
-        def on_scalar(c, b):
-            return 2 * c + b >= WB and (WBONLY == 2 or b == WBONLY) and 2 * c + b < 2 * chunks - 1
+        def weigh_on_scalar(n):
+            width = WIDTHS[n // 2]
+            for i in range(PACK):
+                cols = slice(width * i, width * (i + 1))
+                nc.scalar.activation(
+                    out=h_rows[n][:, cols], in_=tanh_d[n][:, cols], func=ACT.Copy, scale=cw_sb[:, n % 2, i : i + 1]
+                )
 
-        def weigh_s(c, b):
-            width = WIDTHS[c]
-            if on_scalar(c, b):
-                for i in range(PACK):
-                    nc.scalar.activation(out=h_rows[c][b][:, width * i : width * (i + 1)], in_=th[c][b][:, width * i : width * (i + 1)], func=ACT.Copy, scale=cw_sb[:, b, i : i + 1])
-
-        def weigh(c, b):
-            if on_scalar(c, b):
-                nc.vector.tensor_copy(out=h_bf[c][b][:].rearrange("p (c e i) -> p c i e", i=PACK, e=4), in_=h_rows[c][b][:].rearrange("p (i c e) -> p c i e", i=PACK, e=4))
-                return
-            nc.vector.tensor_tensor(
-                out=h_bf[c][b][:].rearrange("p (c e i) -> p c i e", i=PACK, e=E),
-                in0=th[c][b][:].rearrange("p (i c e) -> p c i e", i=PACK, e=E),
-                in1=cw_ps[:, PACK * b : PACK * (b + 1)].unsqueeze(1).unsqueeze(3).to_broadcast([P, WIDTHS[c] // E, PACK, E]),
-                op=ALU.mult,
-            )
-
-        y = {}
+        def weigh(n):
+            if n in SCALAR_WEIGHS:
+                nc.vector.tensor_copy(
+                    out=h_bf[n][:].rearrange("p (r e i) -> p r i e", i=PACK, e=4),
+                    in_=h_rows[n][:].rearrange("p (i r e) -> p r i e", i=PACK, e=4),
+                )
+            else:
+                factor = cw_ps[:, PACK * (n % 2) : PACK * (n % 2 + 1)].unsqueeze(1).unsqueeze(3)
+                nc.vector.tensor_tensor(
+                    out=words_of(h_bf[n][:]),
+                    in0=rows_of(tanh_d[n][:]),
+                    in1=factor.to_broadcast([P, WIDTHS[n // 2] // PAIR, PACK, PAIR]),
+                    op=ALU.mult,
+                )
 
         def outputs(c):
             width = WIDTHS[c]
-            y[c] = y_psum.tile([P, 2, 256], F32, name="y")
+            y[c] = y_psum.tile([P, 2, BANK // 2], F32, name="y")
             for g in range(2):
-                mixed_product(
-                    y[c][:, g, :width],
-                    width,
-                    v8[:, P * g : P * (g + 1)],
-                    v4[:, 2 * P * g : 2 * P * (g + 1)],
-                    v_sc,
-                    P * g,
-                    h_q[c],
-                    h_sc[c],
+                v_scales = v_sc[:, P * g : P * (g + 1)]
+                fp8_pass(y[c][:, g, :width], v8[:, P * g : P * (g + 1)], v_scales, h_q[2 * c], h_sc[2 * c], g == 0)
+            for g in range(2):
+                v_scales = v_sc[:, P * g : P * (g + 1)]
+                fp4_passes(
+                    y[c][:, g, :width], width, v4[:, 2 * P * g : 2 * P * (g + 1)], v_scales, h_q[2 * c + 1], h_sc[2 * c + 1], g == 1
                 )
 
         def add_residual(c):
-            r = 0 if c < RES_SPLIT else 1
-            t0 = starts[c] - res_edges[r]
+            r = min(c, 1)
+            t0 = STARTS[c] - res_edges[r]
             nc.vector.tensor_tensor(
                 out=out_sb[c][:], in0=y[c][:, :, : WIDTHS[c]], in1=res_sb[r][:, :, t0 : t0 + WIDTHS[c]], op=ALU.add
             )
-            nc.sync.dma_start(
-                out=out[:, starts[c] : starts[c + 1]].rearrange("(g p) t -> p g t", p=P), in_=out_sb[c][:]
-            )
+            nc.sync.dma_start(out=out[:, STARTS[c] : STARTS[c + 1]].rearrange("(g p) t -> p g t", p=P), in_=out_sb[c][:])
 
         nc.vector.memset(w_sc_raw[:].bitcast(I32), 0)
         nc.vector.memset(warm_in[:], 0.0)
         nc.vector.memset(v_sc[:].bitcast(I32), 0)
-        nc.vector.memset(cw_pad[:], 0.0)
+        nc.vector.memset(cw_square[:], 0.0)
         nc.scalar.activation(out=warm_out[:], in_=warm_in[:], func=ACT.Tanh)
 
-        def load_w4(b):
-            nc.sync.dma_start(out=w4_raw[b][:].bitcast(I32), in_=w4_words[0][:, 2 * PASS * b : 2 * PASS * (b + 1)].bitcast(I32))
-
-        small = [lambda: nc.sync.dma_start(out=cb_sb[:], in_=cb.rearrange("(b p i) -> p b i", b=2, i=PACK)),
-                 lambda: nc.sync.dma_start(out=cw_sb, in_=cw.rearrange("(b p i) -> p b i", b=2, i=PACK))]
-        load_x(0, 0)
+        load_x(0)
         load_w4(0)
-        for q in range(4):
-            load_scales(w_sc_raw, 0, w4_scales, q, nc.sync)
-        for q in range(4):
-            load_scales(w_sc_raw, FP8_ROW, w8_scales, q, nc.gpsimd if q < GS else nc.sync)
+        for quad in range(QUADS):
+            load_scales(nc.sync, w_sc_raw, 0, w4_scales, quad)
+        for quad in range(QUADS):
+            load_scales(nc.gpsimd if quad < GPSIMD_SCALE_LOADS else nc.sync, w_sc_raw, FP8_ROW, w8_scales, quad)
         make_identity(nc, ident[:])
-        load_x(0, 1)
+        load_x(1)
         load_w8(0)
-        small[0]()
-        small[1]()
+        nc.sync.dma_start(out=cb_sb[:], in_=cb.rearrange("(b p i) -> p b i", b=2, i=PACK))
+        nc.sync.dma_start(out=cw_sb, in_=cw.rearrange("(b p i) -> p b i", b=2, i=PACK))
         load_w4(1)
         load_w8(1)
-        for n in range(2, 2 * chunks):
-            load_x(n // 2, n % 2)
-            if 2 <= n < 6:
-                load_scales(v_sc, FP8_ROW, v8_scales, n - 2, nc.sync)
-                load_scales(v_sc, 0, v4_scales, n - 2, nc.sync)
-            if n == 5:
-                nc.sync.dma_start(out=v8[:].bitcast(I32), in_=v8_words[0].rearrange("p n i -> p (n i)").bitcast(I32))
-                nc.sync.dma_start(out=v4[:].bitcast(I32), in_=v4_words[0].bitcast(I32))
-            if n == RESAT:
-                load_res(0)
-        load_res(1)
+        for quad in range(QUADS):
+            load_x(2 + quad)
+            load_scales(nc.sync, v_sc, FP8_ROW, v8_scales, quad)
+            load_scales(nc.sync, v_sc, 0, v4_scales, quad)
+        nc.sync.dma_start(out=v8[:].bitcast(I32), in_=v8_words[0].rearrange("p n i -> p (n i)").bitcast(I32))
+        nc.sync.dma_start(out=v4[:].bitcast(I32), in_=v4_words[0].bitcast(I32))
+        for n in range(2 + QUADS, STEPS):
+            load_x(n)
+        for r in range(2):
+            nc.sync.dma_start(
+                out=res_sb[r][:], in_=res[:, res_edges[r] : res_edges[r + 1]].rearrange("(g p) t -> p g t", p=P)
+            )
 
-        def warm_pe(count):
-            if count:
-                idle = y_psum.tile([P, 2, 256], F32, name="y")
-                for k in range(count):
-                    nc.tensor.matmul_mx(
-                        out=idle[:, 0, :],
-                        lhsT=x_q[0][0][:, :P].bitcast(FP8X4),
-                        lhsT_scale=x_sc[0][0][:, :P],
-                        rhs=x_q[0][0][:].bitcast(FP8X4),
-                        rhs_scale=x_sc[0][0][:],
-                        start=True,
-                        stop=True,
-                    )
-
-        def quantize_x(n):
-            if n < 2 * chunks:
-                quantize(x_q[n // 2][n % 2], x_sc[n // 2][n % 2], x_bf[n // 2, n % 2])
-
-        def quantize_h(n):
-            quantize(h_q[n // 2][n % 2], h_sc[n // 2][n % 2], h_bf[n // 2][n % 2])
-
-        def ix(n, v):
-            if n < 2 * chunks:
-                interleave_x(n // 2, n % 2, v)
-
-        ix(0, False)
-        ix(0, True)
-        order_w4(0)
+        stage(0, False)
+        interleave("scalar", 0, VECTOR_COLS[0], WIDTHS[0])
+        interleave("vector", 0, 0, VECTOR_COLS[0])
+        gather_w4(0)
         quantize_x(0)
-        warm_pe(WARM0)
-        ix(1, False)
-        ix(1, True)
-        order_w_scales(0)
-        order_w8(0)
+        idle = y_psum.tile([P, 2, BANK // 2], F32, name="y")
+        for repeat in range(WARM_PASSES):
+            nc.tensor.matmul_mx(
+                out=idle[:, 0, :],
+                lhsT=x_q[0][:, :P].bitcast(FP8X4),
+                lhsT_scale=x_sc[0][:, :P],
+                rhs=x_q[0][:].bitcast(FP8X4),
+                rhs_scale=x_sc[0][:],
+                start=True,
+                stop=True,
+            )
+        stage(1, False)
+        interleave("scalar", 1, VECTOR_COLS[1], WIDTHS[0])
+        interleave("vector", 1, 0, VECTOR_COLS[1])
+        gather_w_scales(0)
+        gather_w8(0)
         quantize_x(1)
-        order_w_scales(1)
-        order_w4(1)
-        order_w8(1)
+        gather_w_scales(1)
+        gather_w4(1)
+        gather_w8(1)
 
-        steps = [(c, b) for c in range(chunks) for b in range(2)]
-        added = 0
-        made = 0
-        for n, (c, b) in enumerate(steps):
-            last = n == len(steps) - 1
-            pieces = [2, 3] if n == 0 else [n + 3]
-            if n != 1:
-                centres(c, b)
-            if n == 0:
-                there = y_psum.tile([P, 2, 256], F32, name="y")
-                nc.tensor.transpose(there[:, 0, :P], cw_pad[:], ident[:])
-                nc.scalar.copy(out=cw_rows[:], in_=there[:, 0, :P])
-            if n == LASTAT:
-                for m in range(G1, 2 * chunks):
-                    ix(m, False)
-            weigh_s(c, b)
-            if 2 * made + 3 + OL <= n:
-                outputs(made)
-                made += 1
-            if n == 0:
-                centres(0, 1)
-                nc.tensor.transpose(cw_ps[:], cw_rows[:], ident[:])
-            if n < PRE:
-                for m in pieces:
-                    ix(m, False)
-                if n > 1:
-                    quantize_h(n - 2)
-                for m in pieces:
-                    ix(m, True)
-                    quantize_x(m)
-                if n + 4 >= G0:
-                    ix(n + 4, 2)
-                weigh(c, b)
-            else:
-                if n + 3 < G1:
-                    ix(n + 3, 0)
-                if n > 1:
-                    quantize_h(n - 2)
-                if n == LASTAT + 1:
-                    for m in range(G1, 2 * chunks):
-                        quantize_x(m)
-                if n + 3 < G1:
-                    quantize_x(n + 3)
-                if n + 4 < G1:
-                    ix(n + 4, 2)
-                if n >= LATE and added < made:
-                    add_residual(added)
-                    added += 1
-                weigh(c, b)
-                if ADD0 <= n < LATE and added < made:
-                    add_residual(added)
-                    added += 1
-        quantize_h(2 * chunks - 2)
-        quantize_h(2 * chunks - 1)
-        while made < chunks:
-            if added < made - 1:
-                add_residual(added)
-                added += 1
-            outputs(made)
-            made += 1
-        while added < chunks:
-            add_residual(added)
-            added += 1
+        centres(0)
+        turned = y_psum.tile([P, 2, BANK // 2], F32, name="y")
+        nc.tensor.transpose(turned[:, 0, :P], cw_square[:], ident[:])
+        nc.scalar.copy(out=cw_turned[:], in_=turned[:, 0, :P])
+        centres(1)
+        nc.tensor.transpose(cw_ps[:], cw_turned[:], ident[:])
+
+        for n in (2, 3):
+            stage(n, n + 1 == FIRST_GPSIMD_PIECE)
+            interleave("vector", n, 0, WIDTHS[1])
+            quantize_x(n)
+
+        for n in range(STEPS):
+            ending, starting = n + FIRST_GPSIMD_PIECE - 1, n + FIRST_GPSIMD_PIECE
+            in_hand = FIRST_GPSIMD_PIECE <= ending <= STEPS - 2
+            if in_hand and WIDTHS[ending // 2] > GPSIMD_COLS:
+                interleave("scalar", ending, 0, WIDTHS[ending // 2] - GPSIMD_COLS)
+            if n in SCALAR_WEIGHS:
+                weigh_on_scalar(n)
+            if 2 <= n + 1 < STEPS:
+                centres(n + 1)
+            chunk_done = n >= 4 and n % 2 == 0
+            if chunk_done:
+                outputs(n // 2 - 2)
+            if n >= 2:
+                quantize_h(n - 2)
+            if in_hand:
+                quantize_x(ending)
+            if starting <= STEPS - 2:
+                stage(starting, True)
+                for m in range(starting, STEPS if starting == STEPS - 2 else starting + 1):
+                    interleave("gpsimd", m, WIDTHS[m // 2] - GPSIMD_COLS, WIDTHS[m // 2])
+            weigh(n)
+            if chunk_done:
+                add_residual(n // 2 - 2)
+
+        quantize_h(STEPS - 2)
+        quantize_h(STEPS - 1)
+        for c in range(CHUNKS - 2, CHUNKS):
+            outputs(c)
+        for c in range(CHUNKS - 2, CHUNKS):
+            add_residual(c)

from contextlib import ExitStack

import concourse.mybir as mybir
from concourse.masks import make_identity

K, J, N, T = 1024, 1024, 256, 1024
FLOPS = 2 * K * J * T + 2 * J * N * T

F32 = mybir.dt.float32
BF16 = mybir.dt.bfloat16
I32 = mybir.dt.int32
U32 = mybir.dt.uint32
U8 = mybir.dt.uint8
FP8X4 = mybir.dt.float8_e4m3fn_x4
FP4X4 = mybir.dt.float4_e2m1fn_x4
ACT = mybir.ActivationFunctionType
ALU = mybir.AluOpType

P = 128
PACK = 4
HALF = P * PACK
BANK = 512
QUADS = 4
FP8_ROW = 4
PAIR = 2

WIDTHS = [256, 256, 256, 128, 128]
CHUNKS = len(WIDTHS)
STEPS = 2 * CHUNKS
STARTS = [sum(WIDTHS[:c]) for c in range(CHUNKS + 1)]
VECTOR_COLS = [64, 128]
GPSIMD_COLS = 128
FIRST_GPSIMD_PIECE = 4
SCALAR_WEIGHS = range(FIRST_GPSIMD_PIECE + 1, STEPS - 1, 2)
GPSIMD_SCALE_LOADS = 3
WARM_PASSES = 6


def tile_mix_kern_outl_tanh_mix_res_kernel(
    tc, x, w8_words, w8_scales, w4_words, w4_scales, cw, cb, v8_words, v8_scales, v4_words, v4_scales, res, out
):
    nc = tc.nc

    with ExitStack() as ctx:
        sb = ctx.enter_context(tc.tile_pool(name="sb", bufs=1))
        d_psum = ctx.enter_context(tc.psum_pool(name="d_psum", bufs=5))
        y_psum = ctx.enter_context(tc.psum_pool(name="y_psum", bufs=2))
        cw_psum = ctx.enter_context(tc.psum_pool(name="cw_psum", bufs=1))
        ctx.enter_context(tc.manual_schedule())

        def keep(name, shape, dtype):
            return sb.tile(shape, dtype, name=name, align_bytes=64)

        def per_step(name, cols, dtype, steps):
            return {n: keep("%s%d" % (name, n), [P, cols * WIDTHS[n // 2]], dtype) for n in steps}

        w8_raw = [keep("w8_raw%d" % b, [P, HALF], U32) for b in range(2)]
        w8 = [keep("w8_%d" % b, [P, HALF], U32) for b in range(2)]
        w4_raw = [keep("w4_raw%d" % b, [P, 2 * HALF], U8) for b in range(2)]
        w4 = [keep("w4_%d" % b, [P, 2 * HALF], U8) for b in range(2)]
        w_sc_raw = keep("w_sc_raw", [P, J], U8)
        w_sc = keep("w_sc", [P, J], U8)
        v8 = keep("v8", [P, N], U32)
        v4 = keep("v4", [P, 2 * N], U8)
        v_sc = keep("v_sc", [P, N], U8)
        cb_sb = keep("cb_sb", [P, 2, PACK], F32)
        cw_square = keep("cw_square", [P, P], F32)
        cw_sb = cw_square[:, : 2 * PACK].rearrange("p (b i) -> p b i", b=2)
        cw_turned = keep("cw_turned", [P, P], F32)
        ident = keep("ident", [P, P], F32)
        cw_ps = cw_psum.tile([P, P], F32, name="cw_ps")
        warm_in = keep("warm_in", [P, 1], F32)
        warm_out = keep("warm_out", [P, 1], F32)

        x_raw = per_step("x_raw", PACK, F32, range(STEPS))
        x_bf = {}
        x_q = per_step("x_q", 1, U32, range(STEPS - 2))
        x_sc = per_step("x_sc", 1, U8, range(STEPS - 2))
        x_q_last = keep("x_q_last", [P, 2 * WIDTHS[-1]], U32)
        x_sc_last = keep("x_sc_last", [P, 2 * WIDTHS[-1]], U8)
        for a in range(2):
            x_q[STEPS - 2 + a] = x_q_last[:, a * WIDTHS[-1] : (a + 1) * WIDTHS[-1]]
            x_sc[STEPS - 2 + a] = x_sc_last[:, a * WIDTHS[-1] : (a + 1) * WIDTHS[-1]]
        tanh_d = per_step("tanh_d", PACK, F32, range(STEPS))
        h_rows = per_step("h_rows", PACK, BF16, SCALAR_WEIGHS)
        h_bf = per_step("h_bf", PACK, BF16, range(STEPS))
        h_q = per_step("h_q", 1, U32, range(STEPS))
        h_sc = per_step("h_sc", 1, U8, range(STEPS))
        res_edges = [0, STARTS[1], T]
        res_sb = [keep("res%d" % r, [P, 2, res_edges[r + 1] - res_edges[r]], F32) for r in range(2)]
        out_sb = [keep("out%d" % c, [P, 2, WIDTHS[c]], F32) for c in range(CHUNKS)]
        y = {}

        def load_scales(queue, tile, row, scales, quad):
            queue.dma_start(
                out=tile[32 * quad + row : 32 * quad + row + 4, :].bitcast(I32),
                in_=scales[0, 4 * quad : 4 * quad + 4, :].bitcast(I32),
            )

        def load_x(n):
            c, a = divmod(n, 2)
            rows = x[a * HALF : (a + 1) * HALF, STARTS[c] : STARTS[c + 1]]
            nc.sync.dma_start(
                out=x_raw[n][:].rearrange("p (i t) -> p i t", i=PACK),
                in_=rows.rearrange("(p i) t -> p i t", i=PACK),
            )

        def load_w8(b):
            words = w8_words[0].rearrange("p j i -> p (j i)")
            nc.sync.dma_start(out=w8_raw[b][:].bitcast(I32), in_=words[:, 4 * HALF * b : 4 * HALF * (b + 1)].bitcast(I32))

        def load_w4(b):
            nc.sync.dma_start(
                out=w4_raw[b][:].bitcast(I32), in_=w4_words[0][:, 2 * HALF * b : 2 * HALF * (b + 1)].bitcast(I32)
            )

        def gather_w8(b):
            nc.vector.tensor_copy(
                out=w8[b][:].bitcast(I32).rearrange("p (i r m) -> p r i m", i=PACK, m=4),
                in_=w8_raw[b][:].bitcast(I32).rearrange("p (r m i) -> p r i m", i=PACK, m=4),
            )

        def gather_w4(b):
            nc.vector.tensor_copy(
                out=w4[b][:].rearrange("p (i r m byte) -> p r i m byte", i=PACK, m=8, byte=2),
                in_=w4_raw[b][:].rearrange("p (r m i byte) -> p r i m byte", i=PACK, m=8, byte=2),
            )

        def gather_w_scales(b):
            cols = slice(HALF * b, HALF * (b + 1))
            nc.vector.tensor_copy(
                out=w_sc[:, cols].rearrange("p (i r m) -> p r i m", i=PACK, m=16),
                in_=w_sc_raw[:, cols].rearrange("p (r m i) -> p r i m", i=PACK, m=16),
            )

        def words_of(tile):
            return tile.rearrange("p (r e i) -> p r i e", i=PACK, e=PAIR)

        def rows_of(tile):
            return tile.rearrange("p (i r e) -> p r i e", i=PACK, e=PAIR)

        def stage(n, shared):
            tag = "x_bf_shared" if shared else "x_bf%d" % n
            pieces = 2 if n == STEPS - 2 else 1
            cols = PACK * WIDTHS[n // 2]
            whole = sb.tile([P, pieces * cols], BF16, name="x_bf%d" % n, tag=tag, align_bytes=64)
            x_bf["whole", n] = whole
            for a in range(pieces):
                x_bf[n + a] = whole[:, a * cols : (a + 1) * cols]

        def interleave(engine, n, t0, t1):
            dst = words_of(x_bf[n])[:, t0 // PAIR : t1 // PAIR]
            src = rows_of(x_raw[n][:])[:, t0 // PAIR : t1 // PAIR]
            if engine == "vector":
                nc.vector.tensor_copy(out=dst, in_=src)
            elif engine == "scalar":
                nc.scalar.copy(out=dst, in_=src)
            else:
                nc.gpsimd.tensor_scalar(out=dst, in0=src, scalar1=1.0, scalar2=0.0, op0=ALU.mult, op1=ALU.add)

        def quantize(codes, scales, values):
            nc.vector.quantize_mx(out=codes[:].bitcast(FP8X4), scales=scales[:], in_=values[:])

        def quantize_x(n):
            if n == STEPS - 2:
                quantize(x_q_last, x_sc_last, x_bf["whole", n])
            else:
                quantize(x_q[n], x_sc[n], x_bf["whole", n])

        def quantize_h(n):
            quantize(h_q[n], h_sc[n], h_bf[n])

        def fp8_pass(acc, weights, w_scales, codes, scales, start):
            nc.tensor.matmul_mx(
                out=acc,
                lhsT=weights.bitcast(FP8X4),
                lhsT_scale=w_scales[FP8_ROW:P, :],
                rhs=codes[:].bitcast(FP8X4),
                rhs_scale=scales[:],
                start=start,
                stop=False,
            )

        def fp4_passes(acc, width, weights, w_scales, codes, scales, stop):
            for t0 in range(0, width, P):
                nc.tensor.matmul_mx(
                    out=acc[:, t0 : t0 + P],
                    lhsT=weights.bitcast(FP4X4),
                    lhsT_scale=w_scales,
                    rhs=codes[:, t0 : t0 + P].bitcast(FP8X4),
                    rhs_scale=scales[:, t0 : t0 + P],
                    start=False,
                    stop=stop and t0 + P == width,
                )

        def centres(n):
            c, b = divmod(n, 2)
            width = WIDTHS[c]
            for i in range(PACK):
                bank = d_psum.tile([P, BANK], F32, name="d")
                d = bank[:, :width]
                w_scales = w_sc[:, HALF * b + P * i : HALF * b + P * (i + 1)]
                fp8_pass(d, w8[b][:, P * i : P * (i + 1)], w_scales, x_q[2 * c], x_sc[2 * c], True)
                fp4_passes(d, width, w4[b][:, 2 * P * i : 2 * P * (i + 1)], w_scales, x_q[2 * c + 1], x_sc[2 * c + 1], True)
                nc.scalar.activation(
                    out=tanh_d[n][:, width * i : width * (i + 1)], in_=d, func=ACT.Tanh, bias=cb_sb[:, b, i : i + 1]
                )

        def weigh_on_scalar(n):
            width = WIDTHS[n // 2]
            for i in range(PACK):
                cols = slice(width * i, width * (i + 1))
                nc.scalar.activation(
                    out=h_rows[n][:, cols], in_=tanh_d[n][:, cols], func=ACT.Copy, scale=cw_sb[:, n % 2, i : i + 1]
                )

        def weigh(n):
            if n in SCALAR_WEIGHS:
                nc.vector.tensor_copy(
                    out=h_bf[n][:].rearrange("p (r e i) -> p r i e", i=PACK, e=4),
                    in_=h_rows[n][:].rearrange("p (i r e) -> p r i e", i=PACK, e=4),
                )
            else:
                factor = cw_ps[:, PACK * (n % 2) : PACK * (n % 2 + 1)].unsqueeze(1).unsqueeze(3)
                nc.vector.tensor_tensor(
                    out=words_of(h_bf[n][:]),
                    in0=rows_of(tanh_d[n][:]),
                    in1=factor.to_broadcast([P, WIDTHS[n // 2] // PAIR, PACK, PAIR]),
                    op=ALU.mult,
                )

        def outputs(c):
            width = WIDTHS[c]
            y[c] = y_psum.tile([P, 2, BANK // 2], F32, name="y")
            for g in range(2):
                v_scales = v_sc[:, P * g : P * (g + 1)]
                fp8_pass(y[c][:, g, :width], v8[:, P * g : P * (g + 1)], v_scales, h_q[2 * c], h_sc[2 * c], g == 0)
            for g in range(2):
                v_scales = v_sc[:, P * g : P * (g + 1)]
                fp4_passes(
                    y[c][:, g, :width], width, v4[:, 2 * P * g : 2 * P * (g + 1)], v_scales, h_q[2 * c + 1], h_sc[2 * c + 1], g == 1
                )

        def add_residual(c):
            r = min(c, 1)
            t0 = STARTS[c] - res_edges[r]
            nc.vector.tensor_tensor(
                out=out_sb[c][:], in0=y[c][:, :, : WIDTHS[c]], in1=res_sb[r][:, :, t0 : t0 + WIDTHS[c]], op=ALU.add
            )
            nc.sync.dma_start(out=out[:, STARTS[c] : STARTS[c + 1]].rearrange("(g p) t -> p g t", p=P), in_=out_sb[c][:])

        nc.vector.memset(w_sc_raw[:].bitcast(I32), 0)
        nc.vector.memset(warm_in[:], 0.0)
        nc.vector.memset(v_sc[:].bitcast(I32), 0)
        nc.vector.memset(cw_square[:], 0.0)
        nc.scalar.activation(out=warm_out[:], in_=warm_in[:], func=ACT.Tanh)

        load_x(0)
        load_w4(0)
        for quad in range(QUADS):
            load_scales(nc.sync, w_sc_raw, 0, w4_scales, quad)
        for quad in range(QUADS):
            load_scales(nc.gpsimd if quad < GPSIMD_SCALE_LOADS else nc.sync, w_sc_raw, FP8_ROW, w8_scales, quad)
        make_identity(nc, ident[:])
        load_x(1)
        load_w8(0)
        nc.sync.dma_start(out=cb_sb[:], in_=cb.rearrange("(b p i) -> p b i", b=2, i=PACK))
        nc.sync.dma_start(out=cw_sb, in_=cw.rearrange("(b p i) -> p b i", b=2, i=PACK))
        load_w4(1)
        load_w8(1)
        for quad in range(QUADS):
            load_x(2 + quad)
            load_scales(nc.sync, v_sc, FP8_ROW, v8_scales, quad)
            load_scales(nc.sync, v_sc, 0, v4_scales, quad)
        nc.sync.dma_start(out=v8[:].bitcast(I32), in_=v8_words[0].rearrange("p n i -> p (n i)").bitcast(I32))
        nc.sync.dma_start(out=v4[:].bitcast(I32), in_=v4_words[0].bitcast(I32))
        for n in range(2 + QUADS, STEPS):
            load_x(n)
        for r in range(2):
            nc.sync.dma_start(
                out=res_sb[r][:], in_=res[:, res_edges[r] : res_edges[r + 1]].rearrange("(g p) t -> p g t", p=P)
            )

        stage(0, False)
        interleave("scalar", 0, VECTOR_COLS[0], WIDTHS[0])
        interleave("vector", 0, 0, VECTOR_COLS[0])
        gather_w4(0)
        quantize_x(0)
        idle = y_psum.tile([P, 2, BANK // 2], F32, name="y")
        for repeat in range(WARM_PASSES):
            nc.tensor.matmul_mx(
                out=idle[:, 0, :],
                lhsT=x_q[0][:, :P].bitcast(FP8X4),
                lhsT_scale=x_sc[0][:, :P],
                rhs=x_q[0][:].bitcast(FP8X4),
                rhs_scale=x_sc[0][:],
                start=True,
                stop=True,
            )
        stage(1, False)
        interleave("scalar", 1, VECTOR_COLS[1], WIDTHS[0])
        interleave("vector", 1, 0, VECTOR_COLS[1])
        gather_w_scales(0)
        gather_w8(0)
        quantize_x(1)
        gather_w_scales(1)
        gather_w4(1)
        gather_w8(1)

        centres(0)
        turned = y_psum.tile([P, 2, BANK // 2], F32, name="y")
        nc.tensor.transpose(turned[:, 0, :P], cw_square[:], ident[:])
        nc.scalar.copy(out=cw_turned[:], in_=turned[:, 0, :P])
        centres(1)
        nc.tensor.transpose(cw_ps[:], cw_turned[:], ident[:])

        for n in (2, 3):
            stage(n, n + 1 == FIRST_GPSIMD_PIECE)
            interleave("vector", n, 0, WIDTHS[1])
            quantize_x(n)

        for n in range(STEPS):
            ending, starting = n + FIRST_GPSIMD_PIECE - 1, n + FIRST_GPSIMD_PIECE
            in_hand = FIRST_GPSIMD_PIECE <= ending <= STEPS - 2
            if in_hand and WIDTHS[ending // 2] > GPSIMD_COLS:
                interleave("scalar", ending, 0, WIDTHS[ending // 2] - GPSIMD_COLS)
            if n in SCALAR_WEIGHS:
                weigh_on_scalar(n)
            if 2 <= n + 1 < STEPS:
                centres(n + 1)
            chunk_done = n >= 4 and n % 2 == 0
            if chunk_done:
                outputs(n // 2 - 2)
            if n >= 2:
                quantize_h(n - 2)
            if in_hand:
                quantize_x(ending)
            if starting <= STEPS - 2:
                stage(starting, True)
                for m in range(starting, STEPS if starting == STEPS - 2 else starting + 1):
                    interleave("gpsimd", m, WIDTHS[m // 2] - GPSIMD_COLS, WIDTHS[m // 2])
            weigh(n)
            if chunk_done:
                add_residual(n // 2 - 2)

        quantize_h(STEPS - 2)
        quantize_h(STEPS - 1)
        for c in range(CHUNKS - 2, CHUNKS):
            outputs(c)
        for c in range(CHUNKS - 2, CHUNKS):
            add_residual(c)
